import numpy as np
import ml_dtypes


def mxq(x, axis, fmt="e4m3"):
    dtype, down = {"e4m3": (ml_dtypes.float8_e4m3fn, 7), "e5m2": (ml_dtypes.float8_e5m2, 14)}[fmt]
    v = np.moveaxis(np.asarray(x, np.float32).astype(ml_dtypes.bfloat16).astype(np.float64), axis, -1)
    blocks = v.reshape(v.shape[:-1] + (-1, 32))
    amax = np.abs(blocks).max(-1, keepdims=True)
    byte = np.maximum(np.where(amax > 0, np.frexp(amax)[1] - 1 + 127, 0) - down, 1)
    scale = np.exp2(byte - 127.0)
    codes = (blocks / scale).astype(np.float32).astype(dtype).astype(np.float64)
    return np.moveaxis((codes * scale).reshape(v.shape), -1, axis)


WIDE = False


def mx_kscale(k):
    if not WIDE:
        return np.ones(k)
    levels = np.array([10, -10, 5, -5, 0])
    if k % 512:
        return np.exp2(np.random.permutation(np.resize(levels, k // 32))).repeat(32)
    a = np.empty((k // 512, 16))
    for p in range(k // 512):
        a[p, :8] = np.random.permutation(np.resize(levels, 8))
        for g in range(8):
            far = levels[np.abs(levels - a[p, g]) >= 10]
            a[p, g + 8] = far[np.random.randint(len(far))]
    return np.exp2(a.ravel()).repeat(32)


def f64(x):
    return np.asarray(x).astype(np.float64)


def striped(idx):
    return np.tile(idx.reshape(-1, 16).T, (8, 1)).astype(np.uint16)


def unstriped(offs):
    return offs[:16].T.reshape(-1).astype(np.int64)


E2M1 = np.array([0.0, 0.5, 1.0, 1.5, 2.0, 3.0, 4.0, 6.0, -0.0, -0.5, -1.0, -1.5, -2.0, -3.0, -4.0, -6.0])


def pack_weight(w, fmt):
    k, n = w.shape
    w = f64(np.asarray(w, np.float32).astype(ml_dtypes.bfloat16)).reshape(k // 32, 32, n)
    amax = np.abs(w).max(1)
    if fmt == "e4m3":
        byte = np.frexp(amax)[1] - 1 + 127 - 7
    else:
        mant, ex = np.frexp(amax / 6.0)
        byte = np.where(mant > 0.5, ex, ex - 1) + 127
    byte = np.clip(np.where(amax > 0, byte, 1), 1, 254)
    scaled = (w * np.exp2(127.0 - byte)[:, None, :]).reshape(k, n).astype(np.float32)
    by_word = np.ascontiguousarray(scaled.reshape(k // 512, 128, 4, n).transpose(0, 1, 3, 2))
    if fmt == "e4m3":
        words = by_word.astype(ml_dtypes.float8_e4m3fn).view(np.uint8)
    else:
        c = by_word.astype(ml_dtypes.float4_e2m1fn).view(np.uint8) & 0xF
        words = (c[..., 0::2] | (c[..., 1::2] << 4)).reshape(k // 512, 128, 2 * n)
    return np.ascontiguousarray(words), np.ascontiguousarray(byte.astype(np.uint8).reshape(k // 512, 16, n))


def unpack_weight(words, scales, fmt):
    g, _, n = scales.shape
    words = np.ascontiguousarray(words).reshape(g, 128, n, -1)
    if fmt == "e4m3":
        vals = words.view(ml_dtypes.float8_e4m3fn).astype(np.float64)
    else:
        nib = np.empty((g, 128, n, 4), np.uint8)
        nib[..., 0::2] = words & 0xF
        nib[..., 1::2] = words >> 4
        vals = E2M1[nib]
    vals = vals * np.repeat(np.exp2(scales.astype(np.float64) - 127.0), 8, axis=1)[..., None]
    return vals.transpose(0, 1, 3, 2).reshape(g * 512, n)


def gelu(v):
    return 0.5 * v * (1.0 + np.tanh(np.sqrt(2.0 / np.pi) * (v + 0.044715 * v**3)))


def bf(x):
    return np.asarray(x, np.float32).astype(ml_dtypes.bfloat16)


def planes(Y):
    n, m = Y.shape
    b = f64(bf(Y)).reshape(n // 32, 32, m)
    amax = np.abs(b).max(1)
    byte = np.clip(np.where(amax > 0, np.frexp(amax)[1] - 1 + 127 - 7, 1), 1, 254)
    codes = (b * np.exp2(127.0 - byte)[:, None, :]).reshape(n, m).astype(np.float32).astype(ml_dtypes.float8_e4m3fn).view(np.uint8)
    words = codes.reshape(n // 512, 128, 4, m).transpose(0, 1, 3, 2)
    return np.ascontiguousarray(words), np.ascontiguousarray(byte.astype(np.uint8).reshape(n // 512, 16, m))


K, T, H, S, T2, P, N = 1024, 4096, 512, 1024, 2048, 1024, 1024

def setup_inputs():
    n = np.random.standard_normal
    s = mx_kscale(K)[:, None]
    u = mx_kscale(H)[:, None]
    tab_words, tab_scales = pack_weight(n((K, T)) * s, "e4m3")
    w2_words, w2_scales = pack_weight(n((K, H)) / np.sqrt(K) / s, "e2m1")
    wo_words, wo_scales = pack_weight(n((H, N)) * np.exp(0.8 * n(N)) / np.sqrt(2 * H) / u, "e4m3")
    return {
        "tab_words": tab_words, "tab_scales": tab_scales,
        "offs": striped(np.random.permutation(T)[:S]),
        "w1": (1.5 * n((K, H)) / np.sqrt(K) / s).astype(np.float32),
        "w2_words": w2_words, "w2_scales": w2_scales,
        "w3": (0.7 * n((K, H)) / np.sqrt(K) / s * u.T).astype(np.float32),
        "gain": (1.2 * np.exp(0.3 * n(H)) * u[:, 0]).astype(np.float32),
        "page0": (0.7 * n((H, T2)) * u).astype(np.float32),
        "wgs": np.exp(0.3 * n((128, S))).astype(np.float32),
        "offs2": striped(np.random.permutation(T2)[:S]),
        "offs3": striped(np.random.permutation(T2)[:P]),
        "offs4": striped(np.random.permutation(T2)[:P]),
        "wo_words": wo_words, "wo_scales": wo_scales,
    }

def reference(tab_words, tab_scales, offs, w1, w2_words, w2_scales, w3, gain, page0, wgs, offs2, offs3, offs4, wo_words, wo_scales):
    v = unpack_weight(tab_words, tab_scales, "e4m3")[:, unstriped(offs)]
    w2 = unpack_weight(w2_words, w2_scales, "e2m1")
    wo = unpack_weight(wo_words, wo_scales, "e4m3")
    a = mxq(f64(w1), 0, "e4m3").T @ v
    ga = 0.5 * a * (1.0 + np.tanh(np.sqrt(2.0 / np.pi) * (a + 0.044715 * a ** 3)))
    b = np.tanh((w2.T @ v) + ga)
    h = (mxq(f64(w3), 0, "e4m3").T @ v) + f64(gain)[:, None] * b
    before = f64(page0)
    page = before.copy()
    page[:, unstriped(offs2)] = np.tile(f64(wgs), (H // 128, 1)) * h
    x = page[:, unstriped(offs3)] - before[:, unstriped(offs4)]
    y = wo.T @ mxq(x, 0, "e4m3")
    words, scales = planes(y)
    return y, words, scales

@@ -1,0 +1,386 @@
+from contextlib import ExitStack
+
+import concourse.mybir as mybir
+from concourse.masks import make_identity
+
+K, T, H, S, T2, M, N = 1024, 4096, 512, 1024, 2048, 1024, 1024
+FLOPS = 2 * (3 * K * H * S + H * N * M)
+
+F32 = mybir.dt.float32
+BF16 = mybir.dt.bfloat16
+I32 = mybir.dt.int32
+U32 = mybir.dt.uint32
+U16 = mybir.dt.uint16
+U8 = mybir.dt.uint8
+FP8X4 = mybir.dt.float8_e4m3fn_x4
+FP4X4 = mybir.dt.float4_e2m1fn_x4
+ACT = mybir.ActivationFunctionType
+MULT = mybir.AluOpType.mult
+ADD = mybir.AluOpType.add
+
+P = 128
+PASSES = K // 512
+ROW_TILES = H // P
+HALF = 512
+CHUNK = 256
+CHUNKS = M // CHUNK
+GROUPS = N // 512
+EARLY = 2
+
+
+def tile_list_treeline_advance_features_kernel(
+    tc, tab_words, tab_scales, offs, w1, w2_words, w2_scales, w3, gain, page0, wgs, offs2, offs3, offs4,
+    wo_words, wo_scales, out_0, out_1, out_2,
+):
+    nc = tc.nc
+    with ExitStack() as ctx:
+        lists = ctx.enter_context(tc.tile_pool(name="lists", bufs=1))
+        held = ctx.enter_context(tc.tile_pool(name="held", bufs=1))
+        ring = ctx.enter_context(tc.tile_pool(name="ring", bufs=2))
+        psum = ctx.enter_context(tc.psum_pool(name="psum", bufs=2))
+
+        def keep(shape, dtype, name, tag=None):
+            return held.tile(shape, dtype, name=name, tag=tag or name, align_bytes=64)
+
+        def turn(shape, dtype, name):
+            return ring.tile(shape, dtype, name=name, tag=name, align_bytes=64)
+
+        def bank(tag):
+            return psum.tile([P, 512], F32, name=tag, tag=tag)
+
+        def load_list(src, name):
+            tile = lists.tile([P, S // 16], U16, name=name)
+            nc.sync.dma_start(tile[:], src)
+            return tile
+
+        tab_sc = keep([P, PASSES, T], U8, "tab_sc")
+        nc.vector.memset(tab_sc[:, 0, :].bitcast(I32), 0)
+        nc.gpsimd.memset(tab_sc[:, 1, :].bitcast(I32), 0)
+        w2_sc = keep([P, PASSES, H], U8, "w2_sc")
+        wo_sc_raw = keep([P, N], U8, "wo_sc_raw")
+        nc.vector.memset(w2_sc[:].rearrange("p a c -> p (a c)").bitcast(I32), 0)
+        nc.vector.memset(wo_sc_raw[:].bitcast(I32), 0)
+        ident = keep([P, P], F32, "ident")
+        make_identity(nc, ident[:])
+
+        def load_scale_rows(tile, scales):
+            for quad in range(4):
+                nc.sync.dma_start(
+                    out=tile[32 * quad : 32 * quad + 4].bitcast(I32),
+                    in_=scales[:, 4 * quad : 4 * quad + 4, :].rearrange("a r c -> r a c").bitcast(I32),
+                )
+
+        def load_table(a):
+            tile = keep([P, T], I32, "tab%d" % a)
+            nc.sync.dma_start(out=tile[:], in_=tab_words[a].rearrange("p t i -> p (t i)").bitcast(I32))
+            return tile
+
+        def load_weight(w, name, q):
+            tile = keep([P, PASSES, 4, P], F32, "%s_raw%d" % (name, q))
+            for a in range(PASSES):
+                rows = w[512 * a : 512 * (a + 1), P * q : P * (q + 1)]
+                nc.sync.dma_start(out=tile[:, a, :, :], in_=rows.rearrange("(p j) c -> p j c", j=4))
+            return tile
+
+        def load_page(q):
+            tile = keep([P, T2], F32, "page%d" % q)
+            nc.sync.dma_start(out=tile[:], in_=page0[P * q : P * (q + 1), :])
+            return tile
+
+        w1_raw, w3_raw, page, wgs_half, tab = [], [], [], [], []
+        idx4 = load_list(offs4, "idx4")
+        page.append(load_page(0))
+        idx1 = load_list(offs, "idx1")
+        load_scale_rows(tab_sc, tab_scales)
+        tab.append(load_table(0))
+        w1_raw.append(load_weight(w1, "w1", 0))
+        w2_w = keep([P, PASSES, 2 * H], U8, "w2_w")
+        nc.sync.dma_start(out=w2_w[:].bitcast(I32), in_=w2_words.rearrange("a p c -> p a c").bitcast(I32))
+        for quad in range(4):
+            nc.sync.dma_start(
+                out=wo_sc_raw[32 * quad : 32 * quad + 4, :].bitcast(I32),
+                in_=wo_scales[0, 4 * quad : 4 * quad + 4, :].bitcast(I32),
+            )
+        tab.append(load_table(1))
+        load_scale_rows(w2_sc, w2_scales)
+        gain_col = keep([P, ROW_TILES], F32, "gain_col")
+        with nc.allow_non_contiguous_dma(reason="one gain a partition"):
+            nc.sync.dma_start(out=gain_col[:], in_=gain.rearrange("(q p) -> p q", p=P))
+        w3_raw.append(load_weight(w3, "w3", 0))
+        idx2 = load_list(offs2, "idx2")
+        for half in range(2):
+            tile = keep([P, HALF], F32, "wgs%d" % half)
+            nc.sync.dma_start(out=tile[:], in_=wgs[:, HALF * half : HALF * (half + 1)])
+            wgs_half.append(tile)
+        for q in range(1, ROW_TILES):
+            w1_raw.append(load_weight(w1, "w1", q))
+            w3_raw.append(load_weight(w3, "w3", q))
+            page.append(load_page(q))
+        idx3 = load_list(offs3, "idx3")
+        wo_raw = keep([P, N], I32, "wo_raw")
+        nc.sync.dma_start(out=wo_raw[:], in_=wo_words[0].rearrange("p n i -> p (n i)").bitcast(I32))
+
+        def fetch_before(q):
+            neg = keep([P, M], F32, "minus_before%d" % q)
+            for half in range(2):
+                nc.vector.tensor_scalar(
+                    out=neg[:, HALF * half : HALF * (half + 1)],
+                    in0=page[q][:].indirect(idx4[:, 32 * half : 32 * (half + 1)]),
+                    scalar1=-1.0, scalar2=0.0, op0=MULT, op1=ADD,
+                )
+            return neg
+
+        minus_before = [fetch_before(0)]
+
+        v_sc, v_w = [], []
+        for a in range(PASSES):
+            tile = keep([P, S], U8, "v_sc%d" % a)
+            nc.vector.tensor_copy(tile[:], tab_sc[:, a, :].indirect(idx1[:]))
+            v_sc.append(tile)
+        for a in range(PASSES):
+            tile = keep([P, S], U32, "v_w%d" % a)
+            pieces = 1 if a == 0 else 2
+            for n in range(pieces):
+                width = S // pieces
+                nc.vector.tensor_copy(
+                    tile[:, width * n : width * (n + 1)],
+                    tab[a][:].bitcast(U32).indirect(idx1[:, width // 16 * n : width // 16 * (n + 1)]),
+                )
+            v_w.append(tile)
+
+        def v_operand(a, cols):
+            return v_w[a][:, cols].bitcast(FP8X4), v_sc[a][:, cols]
+
+        def quantise_weight(raw, name, q, on_vector):
+            rounded = keep([P, PASSES, P, 4], BF16, "%s_bf%d" % (name, q))
+            dst = rounded[:].rearrange("p a (c i) j -> p a c j i", i=4)
+            src = raw[:].rearrange("p a j (c i) -> p a c j i", i=4)
+            if on_vector:
+                nc.vector.tensor_copy(out=dst, in_=src)
+            else:
+                nc.scalar.copy(out=dst, in_=src)
+            codes = keep([P, PASSES * P], U32, "%s_codes%d" % (name, q))
+            scales = keep([P, PASSES * P], U8, "%s_scales%d" % (name, q))
+            nc.vector.quantize_mx(
+                out=codes[:].bitcast(FP8X4), scales=scales[:], in_=rounded[:].rearrange("p a c j -> p (a c j)")
+            )
+            return [(codes[:, P * a : P * (a + 1)].bitcast(FP8X4), scales[:, P * a : P * (a + 1)]) for a in range(PASSES)]
+
+        def w2_operand(q):
+            return [
+                (w2_w[:, a, 2 * P * q : 2 * P * (q + 1)].bitcast(FP4X4), w2_sc[:, a, P * q : P * (q + 1)])
+                for a in range(PASSES)
+            ]
+
+        def product_rows(out, weight, j0, width):
+            cols = slice(j0, j0 + width)
+            for a in range(PASSES):
+                codes, scale = v_operand(a, cols)
+                nc.tensor.matmul_mx(
+                    out=out[:, 0:width], lhsT=weight[a][0], lhsT_scale=weight[a][1], rhs=codes, rhs_scale=scale,
+                    start=(a == 0), stop=(a == PASSES - 1),
+                )
+
+        def product_turned(out, weight, j0):
+            for jt in range(HALF // P):
+                cols = slice(j0 + P * jt, j0 + P * (jt + 1))
+                for a in range(PASSES):
+                    codes, scale = v_operand(a, cols)
+                    nc.tensor.matmul_mx(
+                        out=out[:, P * jt : P * (jt + 1)], lhsT=codes, lhsT_scale=scale,
+                        rhs=weight[a][0], rhs_scale=weight[a][1], start=(a == 0), stop=(a == PASSES - 1),
+                    )
+
+        def transposed_sum(out, parts):
+            for n, (block, src) in enumerate(parts):
+                nc.tensor.matmul(
+                    out=out[:, P * block : P * (block + 1)], lhsT=src, rhs=ident[:], is_transpose=True,
+                    start=(n == 0), stop=(n == len(parts) - 1),
+                )
+
+        def inner_tanh(q, j0, width, w1_q):
+            first, second = bank("first"), bank("second")
+            ga = turn([P, width], F32, "ga")
+            other = turn([P, width], F32, "other")
+            b = turn([P, width], F32, "b")
+            if width < HALF:
+                product_rows(first, w1_q, j0, width)
+                product_rows(second, w2_operand(q), j0, width)
+                nc.scalar.activation(out=ga[:], in_=first[:, 0:width], func=ACT.Gelu_apprx_tanh)
+                nc.vector.tensor_tensor(other[:], second[:, 0:width], ga[:], ADD)
+                nc.scalar.activation(out=b[:], in_=other[:], func=ACT.Tanh)
+            else:
+                product_turned(first, w1_q, j0)
+                product_turned(second, w2_operand(q), j0)
+                nc.scalar.activation(out=ga[:], in_=first[:], func=ACT.Gelu_apprx_tanh)
+                nc.scalar.copy(out=other[:], in_=second[:])
+                total = bank("total")
+                blocks = range(HALF // P)
+                transposed_sum(
+                    total,
+                    [(jt, ga[:, P * jt : P * (jt + 1)]) for jt in blocks]
+                    + [(jt, other[:, P * jt : P * (jt + 1)]) for jt in blocks],
+                )
+                nc.scalar.activation(out=b[:], in_=total[:], func=ACT.Tanh)
+            return b
+
+        after = [None] * CHUNKS
+        after_early = keep([P, ROW_TILES, EARLY * CHUNK], F32, "after_early", tag="tab0")
+        x_turned = [keep([P, CHUNK // P, 2, P, 2], BF16, "x_turned%d" % c) for c in range(EARLY)]
+
+        def fetch_after(dst, m0, width, q):
+            nc.vector.tensor_copy(dst, page[q][:].indirect(idx3[:, m0 // 16 : (m0 + width) // 16]))
+
+        def difference_one(q, chunks):
+            m0, width = CHUNK * chunks[0], CHUNK * len(chunks)
+            fetch_after(after_early[:, q, m0 : m0 + width], m0, width, q)
+            total = bank("total")
+            tiles = range(width // P)
+            transposed_sum(
+                total,
+                [(mt, minus_before[q][:, m0 + P * mt : m0 + P * (mt + 1)]) for mt in tiles]
+                + [(mt, after_early[:, q, m0 + P * mt : m0 + P * (mt + 1)]) for mt in tiles],
+            )
+            for n, c in enumerate(chunks):
+                nc.scalar.copy(
+                    out=x_turned[c][:, :, :, 32 * q : 32 * (q + 1), :],
+                    in_=total[:, CHUNK * n : CHUNK * (n + 1)].rearrange("m (mt p u e) -> m mt u p e", mt=CHUNK // P, u=2, e=2),
+                )
+
+        def early_chunks(q):
+            if q + 1 < ROW_TILES:
+                difference_one(q, list(range(EARLY)))
+            else:
+                for c in range(EARLY):
+                    difference_one(q, [c])
+
+        def difference_all(c):
+            x_turned.append(keep([P, CHUNK // P, 2, P, 2], BF16, "x_turned%d" % c, tag="x_turned%d" % (EARLY - 1)))
+            for mt in range(CHUNK // P):
+                total = bank("total")
+                m0 = CHUNK * c + P * mt
+                transposed_sum(
+                    total,
+                    [(q, minus_before[q][:, m0 : m0 + P]) for q in range(ROW_TILES)]
+                    + [(q, after[c][:, q, P * mt : P * (mt + 1)]) for q in range(ROW_TILES)],
+                )
+                nc.scalar.copy(out=x_turned[c][:, mt], in_=total[:].rearrange("m (p u e) -> m u p e", u=2, e=2))
+
+        w1_q = [quantise_weight(w1_raw[0], "w1", 0, False)]
+        wo_sc = keep([P, N], U8, "wo_sc")
+        nc.vector.tensor_copy(
+            out=wo_sc[:].rearrange("p (g t n) -> p g n t", g=GROUPS, t=4),
+            in_=wo_sc_raw[:].rearrange("p (g n t) -> p g n t", g=GROUPS, t=4),
+        )
+        w3_q = [quantise_weight(w3_raw[0], "w3", 0, True)]
+        for q in range(ROW_TILES):
+            pieces = [(0, HALF // 2), (HALF // 2, HALF // 2), (HALF, HALF)] if q == 0 else [(0, HALF), (HALF, HALF)]
+
+            def products(j0, width):
+                b = inner_tanh(q, j0, width, w1_q[q])
+                third = bank("third")
+                product_rows(third, w3_q[q], j0, width)
+                return b, third
+
+            def put(j0, width, b, third, held_back):
+                if held_back:
+                    w1_q.append(quantise_weight(w1_raw[q + 1], "w1", q + 1, False))
+                    w3_q.append(quantise_weight(w3_raw[q + 1], "w3", q + 1, False))
+                    h = keep([P, width], F32, "h_late%d" % q, tag="w1_bf%d" % (q + 1))
+                else:
+                    h = turn([P, width], F32, "h")
+                nc.vector.scalar_tensor_tensor(
+                    out=h[:], in0=b[:], scalar=gain_col[:, q : q + 1], in1=third[:, 0:width], op0=MULT, op1=ADD
+                )
+                w0 = j0 % HALF
+                nc.vector.tensor_tensor(
+                    page[q][:].indirect(idx2[:, j0 // 16 : (j0 + width) // 16]), h[:],
+                    wgs_half[j0 // HALF][:, w0 : w0 + width], MULT,
+                )
+
+            made = [products(*piece) for piece in pieces[:2]]
+            if q > 0:
+                early_chunks(q - 1)
+                minus_before.append(fetch_before(q))
+            for n, piece in enumerate(pieces):
+                put(*piece, *made[n], n == (2 if q == 0 else 0) and q + 1 < ROW_TILES)
+                if n + 2 < len(pieces):
+                    made.append(products(*pieces[n + 2]))
+            if q == 1:
+                wo_w = keep([P, N], I32, "wo_w")
+                nc.vector.tensor_copy(
+                    out=wo_w[:].rearrange("p (g t n) -> p g n t", g=GROUPS, t=4),
+                    in_=wo_raw[:].rearrange("p (g n t) -> p g n t", g=GROUPS, t=4),
+                )
+        early_chunks(ROW_TILES - 1)
+
+        y_sc = keep([P, GROUPS, M], U8, "y_sc")
+        raw_tags = ["w%d_raw%d" % (w, q) for q in range(ROW_TILES) for w in (1, 3)]
+
+        def late_chunk(c, tag):
+            after[c] = keep([P, ROW_TILES, CHUNK], F32, "after%d" % c, tag=tag)
+            for q in range(ROW_TILES):
+                fetch_after(after[c][:, q, :], CHUNK * c, CHUNK, q)
+
+        def quantise_x(c):
+            if c >= EARLY:
+                difference_all(c)
+            pairs = bank("third")
+            words = x_turned[c][:].rearrange("m mt u p e -> m (mt u p e)").bitcast(F32)
+            for n in range(2 * CHUNK // P):
+                nc.tensor.transpose(pairs[:, P * n : P * (n + 1)], words[:, P * n : P * (n + 1)], ident[:])
+            x_bf = keep([P, CHUNK * 4], BF16, "x_bf%d" % c)
+            nc.scalar.copy(
+                out=x_bf[:].bitcast(F32).rearrange("p (mt m u) -> p mt m u", u=2, m=P),
+                in_=pairs[:].rearrange("p (mt u m) -> p mt m u", u=2, m=P),
+            )
+            codes = turn([P, CHUNK], U32, "x_codes")
+            scales = turn([P, CHUNK], U8, "x_scales")
+            nc.vector.quantize_mx(out=codes[:].bitcast(FP8X4), scales=scales[:], in_=x_bf[:])
+            return codes, scales
+
+        def last_product(c, codes, scales):
+            cols = slice(CHUNK * c, CHUNK * (c + 1))
+            for g in range(GROUPS):
+                y = keep([P, 4, CHUNK], F32, "y%d_%d" % (c, g), tag=raw_tags[GROUPS * c + g])
+                for mt in range(CHUNK // P):
+                    acc = bank("first" if mt == 0 else "second")
+                    for t in range(4):
+                        n0 = 512 * g + P * t
+                        nc.tensor.matmul_mx(
+                            out=acc[:, P * t : P * (t + 1)],
+                            lhsT=wo_w[:, n0 : n0 + P].bitcast(FP8X4), lhsT_scale=wo_sc[:, n0 : n0 + P],
+                            rhs=codes[:, P * mt : P * (mt + 1)].bitcast(FP8X4), rhs_scale=scales[:, P * mt : P * (mt + 1)],
+                            start=True, stop=True,
+                        )
+                    nc.scalar.copy(out=y[:, :, P * mt : P * (mt + 1)], in_=acc[:].rearrange("p (t m) -> p t m", t=4))
+                nc.sync.dma_start(
+                    out=out_0[512 * g : 512 * (g + 1), cols].rearrange("(p t) m -> p t m", t=4), in_=y[:]
+                )
+                y_bf = turn([P, CHUNK, 4], BF16, "y_bf")
+                nc.vector.tensor_copy(
+                    out=y_bf[:].rearrange("p (c i) t -> p c t i", i=4),
+                    in_=y[:].rearrange("p t (c i) -> p c t i", i=4),
+                )
+                y_codes = keep([P, CHUNK], U32, "y_codes%d_%d" % (c, g))
+                nc.vector.quantize_mx(
+                    out=y_codes[:].bitcast(FP8X4), scales=y_sc[:, g, cols], in_=y_bf[:].rearrange("p m t -> p (m t)")
+                )
+                nc.sync.dma_start(
+                    out=out_1[g, :, cols, :].rearrange("p m t -> p (m t)").bitcast(I32), in_=y_codes[:].bitcast(I32)
+                )
+
+        late_chunk(EARLY, "wgs1")
+        quantised = []
+        for c in range(CHUNKS):
+            quantised.append(quantise_x(c))
+            if c == 0:
+                late_chunk(EARLY + 1, "x_bf0")
+            if c >= 1:
+                last_product(c - 1, *quantised[c - 1])
+        last_product(CHUNKS - 1, *quantised[CHUNKS - 1])
+        for quad in range(4):
+            nc.sync.dma_start(
+                out=out_2[:, 4 * quad : 4 * quad + 4, :].rearrange("g r m -> r g m").bitcast(I32),
+                in_=y_sc[32 * quad : 32 * quad + 4, :, :].bitcast(I32),
+            )

@@ -53,9 +53,11 @@ def tile_list_treeline_advance_features_kernel(
             nc.sync.dma_start(tile[:], src)
             return tile
 
-        tab_sc = keep([P, PASSES, T], U8, "tab_sc")
-        nc.vector.memset(tab_sc[:, 0, :].bitcast(I32), 0)
-        nc.gpsimd.memset(tab_sc[:, 1, :].bitcast(I32), 0)
+        tab_sc = keep([P, T], U8, "tab_sc")
+        nc.vector.memset(tab_sc[:, 0 : T // 2].bitcast(I32), 0)
+        nc.gpsimd.memset(tab_sc[:, T // 2 : T].bitcast(I32), 0)
+        v_sc1 = keep([P, S], U8, "v_sc1")
+        nc.vector.memset(v_sc1[:].bitcast(I32), 0)
         w2_sc = keep([P, PASSES, H], U8, "w2_sc")
         wo_sc_raw = keep([P, N], U8, "wo_sc_raw")
         nc.vector.memset(w2_sc[:].rearrange("p a c -> p (a c)").bitcast(I32), 0)
@@ -87,15 +89,17 @@ def tile_list_treeline_advance_features_kernel(
             nc.sync.dma_start(out=tile[:], in_=page0[P * q : P * (q + 1), :])
             return tile
 
-        w1_raw, w3_raw, page, wgs_half, tab = [], [], [], [], []
-        idx4 = load_list(offs4, "idx4")
-        page.append(load_page(0))
+        w1_raw, w3_raw, page, tab = [], [], [], []
         idx1 = load_list(offs, "idx1")
-        load_scale_rows(tab_sc, tab_scales)
-        tab.append(load_table(0))
-        w1_raw.append(load_weight(w1, "w1", 0))
         w2_w = keep([P, PASSES, 2 * H], U8, "w2_w")
         nc.sync.dma_start(out=w2_w[:].bitcast(I32), in_=w2_words.rearrange("a p c -> p a c").bitcast(I32))
+        for quad in range(4):
+            nc.sync.dma_start(
+                out=tab_sc[32 * quad : 32 * quad + 8, :].bitcast(I32),
+                in_=tab_scales[:, 4 * quad : 4 * quad + 4, :].bitcast(I32),
+            )
+        tab.append(load_table(0))
+        w1_raw.append(load_weight(w1, "w1", 0))
         for quad in range(4):
             nc.sync.dma_start(
                 out=wo_sc_raw[32 * quad : 32 * quad + 4, :].bitcast(I32),
@@ -103,15 +107,17 @@ def tile_list_treeline_advance_features_kernel(
             )
         tab.append(load_table(1))
         load_scale_rows(w2_sc, w2_scales)
+        w3_raw.append(load_weight(w3, "w3", 0))
+        page.append(load_page(0))
+        idx4 = load_list(offs4, "idx4")
         gain_col = keep([P, ROW_TILES], F32, "gain_col")
         with nc.allow_non_contiguous_dma(reason="one gain a partition"):
             nc.sync.dma_start(out=gain_col[:], in_=gain.rearrange("(q p) -> p q", p=P))
-        w3_raw.append(load_weight(w3, "w3", 0))
         idx2 = load_list(offs2, "idx2")
+        wgs_sb = keep([P, S], F32, "wgs_sb")
         for half in range(2):
-            tile = keep([P, HALF], F32, "wgs%d" % half)
-            nc.sync.dma_start(out=tile[:], in_=wgs[:, HALF * half : HALF * (half + 1)])
-            wgs_half.append(tile)
+            cols = slice(HALF * half, HALF * (half + 1))
+            nc.sync.dma_start(out=wgs_sb[:, cols], in_=wgs[:, cols])
         for q in range(1, ROW_TILES):
             w1_raw.append(load_weight(w1, "w1", q))
             w3_raw.append(load_weight(w3, "w3", q))
@@ -130,13 +136,12 @@ def tile_list_treeline_advance_features_kernel(
                 )
             return neg
 
-        minus_before = [fetch_before(0)]
+        minus_before = []
 
-        v_sc, v_w = [], []
-        for a in range(PASSES):
-            tile = keep([P, S], U8, "v_sc%d" % a)
-            nc.vector.tensor_copy(tile[:], tab_sc[:, a, :].indirect(idx1[:]))
-            v_sc.append(tile)
+        v_sc = keep([P, S], U8, "v_sc")
+        nc.vector.tensor_copy(v_sc[:], tab_sc[:].indirect(idx1[:]))
+        nc.gpsimd.dma_start(out=v_sc1[0 : P - 4, :].bitcast(I32), in_=v_sc[4:P, :].bitcast(I32))
+        v_w = []
         for a in range(PASSES):
             tile = keep([P, S], U32, "v_w%d" % a)
             pieces = 1 if a == 0 else 2
@@ -148,8 +153,9 @@ def tile_list_treeline_advance_features_kernel(
                 )
             v_w.append(tile)
 
-        def v_operand(a, cols):
-            return v_w[a][:, cols].bitcast(FP8X4), v_sc[a][:, cols]
+        def v_operand(a, cols, partner):
+            scale = v_sc1[:, cols] if (a == 1 and partner.dtype == FP4X4) else v_sc[4 * a : P, cols]
+            return v_w[a][:, cols].bitcast(FP8X4), scale
 
         def quantise_weight(raw, name, q, on_vector):
             rounded = keep([P, PASSES, P, 4], BF16, "%s_bf%d" % (name, q))
@@ -175,7 +181,7 @@ def tile_list_treeline_advance_features_kernel(
         def product_rows(out, weight, j0, width):
             cols = slice(j0, j0 + width)
             for a in range(PASSES):
-                codes, scale = v_operand(a, cols)
+                codes, scale = v_operand(a, cols, weight[a][0])
                 nc.tensor.matmul_mx(
                     out=out[:, 0:width], lhsT=weight[a][0], lhsT_scale=weight[a][1], rhs=codes, rhs_scale=scale,
                     start=(a == 0), stop=(a == PASSES - 1),
@@ -185,7 +191,7 @@ def tile_list_treeline_advance_features_kernel(
             for jt in range(HALF // P):
                 cols = slice(j0 + P * jt, j0 + P * (jt + 1))
                 for a in range(PASSES):
-                    codes, scale = v_operand(a, cols)
+                    codes, scale = v_operand(a, cols, weight[a][0])
                     nc.tensor.matmul_mx(
                         out=out[:, P * jt : P * (jt + 1)], lhsT=codes, lhsT_scale=scale,
                         rhs=weight[a][0], rhs_scale=weight[a][1], start=(a == 0), stop=(a == PASSES - 1),
@@ -200,7 +206,10 @@ def tile_list_treeline_advance_features_kernel(
 
         def inner_tanh(q, j0, width, w1_q):
             first, second = bank("first"), bank("second")
-            ga = turn([P, width], F32, "ga")
+            if width < HALF and j0 > 0:
+                ga = keep([P, width], F32, "ga_late", tag="minus_before0")
+            else:
+                ga = turn([P, width], F32, "other" if (q == 0 and j0 > 0) else "ga")
             other = turn([P, width], F32, "other")
             b = turn([P, width], F32, "b")
             if width < HALF:
@@ -257,7 +266,7 @@ def tile_list_treeline_advance_features_kernel(
         def difference_all(c):
             x_turned.append(keep([P, CHUNK // P, 2, P, 2], BF16, "x_turned%d" % c, tag="x_turned%d" % (EARLY - 1)))
             for mt in range(CHUNK // P):
-                total = bank("total")
+                total = bank("third" if c == EARLY else "total")
                 m0 = CHUNK * c + P * mt
                 transposed_sum(
                     total,
@@ -282,30 +291,36 @@ def tile_list_treeline_advance_features_kernel(
                 product_rows(third, w3_q[q], j0, width)
                 return b, third
 
-            def put(j0, width, b, third, held_back):
+            def put(group, held_back):
+                j0, width = group[0][0], sum(piece[1] for piece in group)
                 if held_back:
                     w1_q.append(quantise_weight(w1_raw[q + 1], "w1", q + 1, False))
                     w3_q.append(quantise_weight(w3_raw[q + 1], "w3", q + 1, False))
                     h = keep([P, width], F32, "h_late%d" % q, tag="w1_bf%d" % (q + 1))
+                elif width == S:
+                    h = keep([P, width], F32, "h_late%d" % q, tag="tab1")
                 else:
                     h = turn([P, width], F32, "h")
-                nc.vector.scalar_tensor_tensor(
-                    out=h[:], in0=b[:], scalar=gain_col[:, q : q + 1], in1=third[:, 0:width], op0=MULT, op1=ADD
-                )
-                w0 = j0 % HALF
+                for start, cols, b, third in group:
+                    nc.vector.scalar_tensor_tensor(
+                        out=h[:, start - j0 : start - j0 + cols], in0=b[:], scalar=gain_col[:, q : q + 1],
+                        in1=third[:, 0:cols], op0=MULT, op1=ADD,
+                    )
                 nc.vector.tensor_tensor(
-                    page[q][:].indirect(idx2[:, j0 // 16 : (j0 + width) // 16]), h[:],
-                    wgs_half[j0 // HALF][:, w0 : w0 + width], MULT,
+                    page[q][:].indirect(idx2[:, j0 // 16 : (j0 + width) // 16]), h[:], wgs_sb[:, j0 : j0 + width], MULT
                 )
 
-            made = [products(*piece) for piece in pieces[:2]]
+            made = [piece + products(*piece) for piece in pieces[:2]]
             if q > 0:
                 early_chunks(q - 1)
-                minus_before.append(fetch_before(q))
-            for n, piece in enumerate(pieces):
-                put(*piece, *made[n], n == (2 if q == 0 else 0) and q + 1 < ROW_TILES)
-                if n + 2 < len(pieces):
-                    made.append(products(*pieces[n + 2]))
+            minus_before.append(fetch_before(q))
+            if q >= 2:
+                put(made, q + 1 < ROW_TILES)
+            else:
+                for n in range(len(pieces)):
+                    put([made[n]], n == 1 - q)
+                    if n + 2 < len(pieces):
+                        made.append(pieces[n + 2] + products(*pieces[n + 2]))
             if q == 1:
                 wo_w = keep([P, N], I32, "wo_w")
                 nc.vector.tensor_copy(
@@ -325,7 +340,7 @@ def tile_list_treeline_advance_features_kernel(
         def quantise_x(c):
             if c >= EARLY:
                 difference_all(c)
-            pairs = bank("third")
+            pairs = bank(("first", "second", "third", "third")[c])
             words = x_turned[c][:].rearrange("m mt u p e -> m (mt u p e)").bitcast(F32)
             for n in range(2 * CHUNK // P):
                 nc.tensor.transpose(pairs[:, P * n : P * (n + 1)], words[:, P * n : P * (n + 1)], ident[:])
@@ -357,20 +372,25 @@ def tile_list_treeline_advance_features_kernel(
                 nc.sync.dma_start(
                     out=out_0[512 * g : 512 * (g + 1), cols].rearrange("(p t) m -> p t m", t=4), in_=y[:]
                 )
-                y_bf = turn([P, CHUNK, 4], BF16, "y_bf")
+                if c % 2 == 0:
+                    y_bf[g] = turn([P, 2 * CHUNK, 4], BF16, "y_bf")
                 nc.vector.tensor_copy(
-                    out=y_bf[:].rearrange("p (c i) t -> p c t i", i=4),
+                    out=y_bf[g][:, CHUNK * (c % 2) : CHUNK * (c % 2 + 1), :].rearrange("p (c i) t -> p c t i", i=4),
                     in_=y[:].rearrange("p t (c i) -> p c t i", i=4),
                 )
-                y_codes = keep([P, CHUNK], U32, "y_codes%d_%d" % (c, g))
-                nc.vector.quantize_mx(
-                    out=y_codes[:].bitcast(FP8X4), scales=y_sc[:, g, cols], in_=y_bf[:].rearrange("p m t -> p (m t)")
-                )
-                nc.sync.dma_start(
-                    out=out_1[g, :, cols, :].rearrange("p m t -> p (m t)").bitcast(I32), in_=y_codes[:].bitcast(I32)
-                )
+                if c % 2 == 1:
+                    both = slice(CHUNK * (c - 1), CHUNK * (c + 1))
+                    y_codes = keep([P, 2 * CHUNK], U32, "y_codes%d_%d" % (c, g))
+                    nc.vector.quantize_mx(
+                        out=y_codes[:].bitcast(FP8X4), scales=y_sc[:, g, both],
+                        in_=y_bf[g][:].rearrange("p m t -> p (m t)"),
+                    )
+                    nc.sync.dma_start(
+                        out=out_1[g, :, both, :].rearrange("p m t -> p (m t)").bitcast(I32), in_=y_codes[:].bitcast(I32)
+                    )
 
-        late_chunk(EARLY, "wgs1")
+        y_bf = [None] * GROUPS
+        late_chunk(EARLY, "wgs_sb")
         quantised = []
         for c in range(CHUNKS):
             quantised.append(quantise_x(c))
@@ -380,7 +400,7 @@ def tile_list_treeline_advance_features_kernel(
                 last_product(c - 1, *quantised[c - 1])
         last_product(CHUNKS - 1, *quantised[CHUNKS - 1])
         for quad in range(4):
-            nc.sync.dma_start(
+            (nc.sync if quad % 2 else nc.scalar).dma_start(
                 out=out_2[:, 4 * quad : 4 * quad + 4, :].rearrange("g r m -> r g m").bitcast(I32),
                 in_=y_sc[32 * quad : 32 * quad + 4, :, :].bitcast(I32),
             )

@@ -56,6 +56,8 @@ def tile_list_treeline_advance_features_kernel(
         tab_sc = keep([P, T], U8, "tab_sc")
         nc.vector.memset(tab_sc[:, 0 : T // 2].bitcast(I32), 0)
         nc.gpsimd.memset(tab_sc[:, T // 2 : T].bitcast(I32), 0)
+        gain_rows = keep([P, P], F32, "gain_rows")
+        nc.vector.memset(gain_rows[:], 0.0)
         v_sc1 = keep([P, S], U8, "v_sc1")
         nc.vector.memset(v_sc1[:].bitcast(I32), 0)
         w2_sc = keep([P, PASSES, H], U8, "w2_sc")
@@ -98,6 +100,7 @@ def tile_list_treeline_advance_features_kernel(
                 out=tab_sc[32 * quad : 32 * quad + 8, :].bitcast(I32),
                 in_=tab_scales[:, 4 * quad : 4 * quad + 4, :].bitcast(I32),
             )
+        nc.sync.dma_start(out=gain_rows[0:ROW_TILES, :], in_=gain.rearrange("(q p) -> q p", p=P))
         tab.append(load_table(0))
         w1_raw.append(load_weight(w1, "w1", 0))
         for quad in range(4):
@@ -110,9 +113,6 @@ def tile_list_treeline_advance_features_kernel(
         w3_raw.append(load_weight(w3, "w3", 0))
         page.append(load_page(0))
         idx4 = load_list(offs4, "idx4")
-        gain_col = keep([P, ROW_TILES], F32, "gain_col")
-        with nc.allow_non_contiguous_dma(reason="one gain a partition"):
-            nc.sync.dma_start(out=gain_col[:], in_=gain.rearrange("(q p) -> p q", p=P))
         idx2 = load_list(offs2, "idx2")
         wgs_sb = keep([P, S], F32, "wgs_sb")
         for half in range(2):
@@ -159,8 +159,8 @@ def tile_list_treeline_advance_features_kernel(
 
         def quantise_weight(raw, name, q, on_vector):
             rounded = keep([P, PASSES, P, 4], BF16, "%s_bf%d" % (name, q))
-            dst = rounded[:].rearrange("p a (c i) j -> p a c j i", i=4)
-            src = raw[:].rearrange("p a j (c i) -> p a c j i", i=4)
+            dst = rounded[:].rearrange("p a (c i) j -> p a c j i", i=2)
+            src = raw[:].rearrange("p a j (c i) -> p a c j i", i=2)
             if on_vector:
                 nc.vector.tensor_copy(out=dst, in_=src)
             else:
@@ -235,53 +235,42 @@ def tile_list_treeline_advance_features_kernel(
 
         after = [None] * CHUNKS
         after_early = keep([P, ROW_TILES, EARLY * CHUNK], F32, "after_early", tag="tab0")
+        for c in range(EARLY):
+            after[c] = after_early[:, :, CHUNK * c : CHUNK * (c + 1)]
         x_turned = [keep([P, CHUNK // P, 2, P, 2], BF16, "x_turned%d" % c) for c in range(EARLY)]
 
         def fetch_after(dst, m0, width, q):
             nc.vector.tensor_copy(dst, page[q][:].indirect(idx3[:, m0 // 16 : (m0 + width) // 16]))
 
-        def difference_one(q, chunks):
-            m0, width = CHUNK * chunks[0], CHUNK * len(chunks)
-            fetch_after(after_early[:, q, m0 : m0 + width], m0, width, q)
-            total = bank("total")
-            tiles = range(width // P)
+        def difference_part(c, mt_list, q_list, tag):
+            total = bank(tag)
+            blocks = [(mt, q) for mt in mt_list for q in q_list]
             transposed_sum(
                 total,
-                [(mt, minus_before[q][:, m0 + P * mt : m0 + P * (mt + 1)]) for mt in tiles]
-                + [(mt, after_early[:, q, m0 + P * mt : m0 + P * (mt + 1)]) for mt in tiles],
+                [(n, minus_before[q][:, CHUNK * c + P * mt : CHUNK * c + P * (mt + 1)]) for n, (mt, q) in enumerate(blocks)]
+                + [(n, after[c][:, q, P * mt : P * (mt + 1)]) for n, (mt, q) in enumerate(blocks)],
             )
-            for n, c in enumerate(chunks):
-                nc.scalar.copy(
-                    out=x_turned[c][:, :, :, 32 * q : 32 * (q + 1), :],
-                    in_=total[:, CHUNK * n : CHUNK * (n + 1)].rearrange("m (mt p u e) -> m mt u p e", mt=CHUNK // P, u=2, e=2),
-                )
-
-        def early_chunks(q):
-            if q + 1 < ROW_TILES:
-                difference_one(q, list(range(EARLY)))
-            else:
-                for c in range(EARLY):
-                    difference_one(q, [c])
+            nc.scalar.copy(
+                out=x_turned[c][:, mt_list[0] : mt_list[-1] + 1, :, 32 * q_list[0] : 32 * (q_list[-1] + 1), :],
+                in_=total[:, 0 : P * len(blocks)].rearrange("m (mt p u e) -> m mt u p e", mt=len(mt_list), u=2, e=2),
+            )
 
         def difference_all(c):
             x_turned.append(keep([P, CHUNK // P, 2, P, 2], BF16, "x_turned%d" % c, tag="x_turned%d" % (EARLY - 1)))
             for mt in range(CHUNK // P):
-                total = bank("third" if c == EARLY else "total")
-                m0 = CHUNK * c + P * mt
-                transposed_sum(
-                    total,
-                    [(q, minus_before[q][:, m0 : m0 + P]) for q in range(ROW_TILES)]
-                    + [(q, after[c][:, q, P * mt : P * (mt + 1)]) for q in range(ROW_TILES)],
-                )
-                nc.scalar.copy(out=x_turned[c][:, mt], in_=total[:].rearrange("m (p u e) -> m u p e", u=2, e=2))
+                difference_part(c, [mt], list(range(ROW_TILES)), "third" if c == EARLY else "total")
 
         w1_q = [quantise_weight(w1_raw[0], "w1", 0, False)]
         wo_sc = keep([P, N], U8, "wo_sc")
         nc.vector.tensor_copy(
-            out=wo_sc[:].rearrange("p (g t n) -> p g n t", g=GROUPS, t=4),
-            in_=wo_sc_raw[:].rearrange("p (g n t) -> p g n t", g=GROUPS, t=4),
+            out=wo_sc[:].rearrange("p (g t c i) -> p g c t i", g=GROUPS, t=4, i=16),
+            in_=wo_sc_raw[:].rearrange("p (g c i t) -> p g c t i", g=GROUPS, t=4, i=16),
         )
         w3_q = [quantise_weight(w3_raw[0], "w3", 0, True)]
+        gain_bank = bank("total")
+        nc.tensor.transpose(gain_bank[:, 0:P], gain_rows[:], ident[:])
+        gain_col = keep([P, ROW_TILES], F32, "gain_col")
+        nc.scalar.copy(out=gain_col[:], in_=gain_bank[:, 0:ROW_TILES])
         for q in range(ROW_TILES):
             pieces = [(0, HALF // 2), (HALF // 2, HALF // 2), (HALF, HALF)] if q == 0 else [(0, HALF), (HALF, HALF)]
 
@@ -312,7 +301,7 @@ def tile_list_treeline_advance_features_kernel(
 
             made = [piece + products(*piece) for piece in pieces[:2]]
             if q > 0:
-                early_chunks(q - 1)
+                fetch_after(after_early[:, q - 1, :], 0, EARLY * CHUNK, q - 1)
             minus_before.append(fetch_before(q))
             if q >= 2:
                 put(made, q + 1 < ROW_TILES)
@@ -324,10 +313,15 @@ def tile_list_treeline_advance_features_kernel(
             if q == 1:
                 wo_w = keep([P, N], I32, "wo_w")
                 nc.vector.tensor_copy(
-                    out=wo_w[:].rearrange("p (g t n) -> p g n t", g=GROUPS, t=4),
-                    in_=wo_raw[:].rearrange("p (g n t) -> p g n t", g=GROUPS, t=4),
+                    out=wo_w[:].rearrange("p (g t c i) -> p g c t i", g=GROUPS, t=4, i=4),
+                    in_=wo_raw[:].rearrange("p (g c i t) -> p g c t i", g=GROUPS, t=4, i=4),
                 )
-        early_chunks(ROW_TILES - 1)
+        for c in range(EARLY):
+            for mt in range(CHUNK // P):
+                difference_part(c, [mt], list(range(ROW_TILES - 1)), "third")
+        for c in range(EARLY):
+            fetch_after(after[c][:, ROW_TILES - 1, :], CHUNK * c, CHUNK, ROW_TILES - 1)
+            difference_part(c, list(range(CHUNK // P)), [ROW_TILES - 1], "total")
 
         y_sc = keep([P, GROUPS, M], U8, "y_sc")
         raw_tags = ["w%d_raw%d" % (w, q) for q in range(ROW_TILES) for w in (1, 3)]
@@ -358,25 +352,24 @@ def tile_list_treeline_advance_features_kernel(
             cols = slice(CHUNK * c, CHUNK * (c + 1))
             for g in range(GROUPS):
                 y = keep([P, 4, CHUNK], F32, "y%d_%d" % (c, g), tag=raw_tags[GROUPS * c + g])
-                for mt in range(CHUNK // P):
-                    acc = bank("first" if mt == 0 else "second")
-                    for t in range(4):
-                        n0 = 512 * g + P * t
+                for pair in range(2):
+                    acc = bank("first" if pair == 0 else "second")
+                    for n in range(2):
+                        n0 = 512 * g + P * (2 * pair + n)
                         nc.tensor.matmul_mx(
-                            out=acc[:, P * t : P * (t + 1)],
+                            out=acc[:, CHUNK * n : CHUNK * (n + 1)],
                             lhsT=wo_w[:, n0 : n0 + P].bitcast(FP8X4), lhsT_scale=wo_sc[:, n0 : n0 + P],
-                            rhs=codes[:, P * mt : P * (mt + 1)].bitcast(FP8X4), rhs_scale=scales[:, P * mt : P * (mt + 1)],
-                            start=True, stop=True,
+                            rhs=codes[:].bitcast(FP8X4), rhs_scale=scales[:], start=True, stop=True,
                         )
-                    nc.scalar.copy(out=y[:, :, P * mt : P * (mt + 1)], in_=acc[:].rearrange("p (t m) -> p t m", t=4))
+                    nc.scalar.copy(out=y[:, 2 * pair : 2 * pair + 2, :].rearrange("p t m -> p (t m)"), in_=acc[:])
                 nc.sync.dma_start(
                     out=out_0[512 * g : 512 * (g + 1), cols].rearrange("(p t) m -> p t m", t=4), in_=y[:]
                 )
                 if c % 2 == 0:
                     y_bf[g] = turn([P, 2 * CHUNK, 4], BF16, "y_bf")
                 nc.vector.tensor_copy(
-                    out=y_bf[g][:, CHUNK * (c % 2) : CHUNK * (c % 2 + 1), :].rearrange("p (c i) t -> p c t i", i=4),
-                    in_=y[:].rearrange("p t (c i) -> p c t i", i=4),
+                    out=y_bf[g][:, CHUNK * (c % 2) : CHUNK * (c % 2 + 1), :].rearrange("p (c i) t -> p c t i", i=2),
+                    in_=y[:].rearrange("p t (c i) -> p c t i", i=2),
                 )
                 if c % 2 == 1:
                     both = slice(CHUNK * (c - 1), CHUNK * (c + 1))

from contextlib import ExitStack

import concourse.mybir as mybir
from concourse.masks import make_identity

K, T, H, S, T2, M, N = 1024, 4096, 512, 1024, 2048, 1024, 1024
FLOPS = 2 * (3 * K * H * S + H * N * M)

F32 = mybir.dt.float32
BF16 = mybir.dt.bfloat16
I32 = mybir.dt.int32
U32 = mybir.dt.uint32
U16 = mybir.dt.uint16
U8 = mybir.dt.uint8
FP8X4 = mybir.dt.float8_e4m3fn_x4
FP4X4 = mybir.dt.float4_e2m1fn_x4
ACT = mybir.ActivationFunctionType
MULT = mybir.AluOpType.mult
ADD = mybir.AluOpType.add

P = 128
PASSES = K // 512
ROW_TILES = H // P
HALF = 512
CHUNK = 256
CHUNKS = M // CHUNK
GROUPS = N // 512
EARLY = 2


def tile_list_treeline_advance_features_kernel(
    tc, tab_words, tab_scales, offs, w1, w2_words, w2_scales, w3, gain, page0, wgs, offs2, offs3, offs4,
    wo_words, wo_scales, out_0, out_1, out_2,
):
    nc = tc.nc
    with ExitStack() as ctx:
        lists = ctx.enter_context(tc.tile_pool(name="lists", bufs=1))
        held = ctx.enter_context(tc.tile_pool(name="held", bufs=1))
        ring = ctx.enter_context(tc.tile_pool(name="ring", bufs=2))
        psum = ctx.enter_context(tc.psum_pool(name="psum", bufs=2))

        def keep(shape, dtype, name, tag=None):
            return held.tile(shape, dtype, name=name, tag=tag or name, align_bytes=64)

        def turn(shape, dtype, name):
            return ring.tile(shape, dtype, name=name, tag=name, align_bytes=64)

        def bank(tag):
            return psum.tile([P, 512], F32, name=tag, tag=tag)

        def load_list(src, name):
            tile = lists.tile([P, S // 16], U16, name=name)
            nc.sync.dma_start(tile[:], src)
            return tile

        tab_sc = keep([P, T], U8, "tab_sc")
        nc.vector.memset(tab_sc[:, 0 : T // 2].bitcast(I32), 0)
        nc.gpsimd.memset(tab_sc[:, T // 2 : T].bitcast(I32), 0)
        gain_rows = keep([P, P], F32, "gain_rows")
        nc.vector.memset(gain_rows[:], 0.0)
        v_sc1 = keep([P, S], U8, "v_sc1")
        nc.vector.memset(v_sc1[:].bitcast(I32), 0)
        w2_sc = keep([P, PASSES, H], U8, "w2_sc")
        wo_sc_raw = keep([P, N], U8, "wo_sc_raw")
        nc.vector.memset(w2_sc[:].rearrange("p a c -> p (a c)").bitcast(I32), 0)
        nc.vector.memset(wo_sc_raw[:].bitcast(I32), 0)
        ident = keep([P, P], F32, "ident")
        make_identity(nc, ident[:])

        def load_scale_rows(tile, scales):
            for quad in range(4):
                nc.sync.dma_start(
                    out=tile[32 * quad : 32 * quad + 4].bitcast(I32),
                    in_=scales[:, 4 * quad : 4 * quad + 4, :].rearrange("a r c -> r a c").bitcast(I32),
                )

        def load_table(a):
            tile = keep([P, T], I32, "tab%d" % a)
            nc.sync.dma_start(out=tile[:], in_=tab_words[a].rearrange("p t i -> p (t i)").bitcast(I32))
            return tile

        def load_weight(w, name, q):
            tile = keep([P, PASSES, 4, P], F32, "%s_raw%d" % (name, q))
            for a in range(PASSES):
                rows = w[512 * a : 512 * (a + 1), P * q : P * (q + 1)]
                nc.sync.dma_start(out=tile[:, a, :, :], in_=rows.rearrange("(p j) c -> p j c", j=4))
            return tile

        def load_page(q):
            tile = keep([P, T2], F32, "page%d" % q)
            nc.sync.dma_start(out=tile[:], in_=page0[P * q : P * (q + 1), :])
            return tile

        w1_raw, w3_raw, page, tab = [], [], [], []
        idx1 = load_list(offs, "idx1")
        w2_w = keep([P, PASSES, 2 * H], U8, "w2_w")
        nc.sync.dma_start(out=w2_w[:].bitcast(I32), in_=w2_words.rearrange("a p c -> p a c").bitcast(I32))
        for quad in range(4):
            nc.sync.dma_start(
                out=tab_sc[32 * quad : 32 * quad + 8, :].bitcast(I32),
                in_=tab_scales[:, 4 * quad : 4 * quad + 4, :].bitcast(I32),
            )
        nc.sync.dma_start(out=gain_rows[0:ROW_TILES, :], in_=gain.rearrange("(q p) -> q p", p=P))
        tab.append(load_table(0))
        w1_raw.append(load_weight(w1, "w1", 0))
        for quad in range(4):
            nc.sync.dma_start(
                out=wo_sc_raw[32 * quad : 32 * quad + 4, :].bitcast(I32),
                in_=wo_scales[0, 4 * quad : 4 * quad + 4, :].bitcast(I32),
            )
        tab.append(load_table(1))
        load_scale_rows(w2_sc, w2_scales)
        w3_raw.append(load_weight(w3, "w3", 0))
        page.append(load_page(0))
        idx4 = load_list(offs4, "idx4")
        idx2 = load_list(offs2, "idx2")
        wgs_sb = keep([P, S], F32, "wgs_sb")
        for half in range(2):
            cols = slice(HALF * half, HALF * (half + 1))
            nc.sync.dma_start(out=wgs_sb[:, cols], in_=wgs[:, cols])
        for q in range(1, ROW_TILES):
            w1_raw.append(load_weight(w1, "w1", q))
            w3_raw.append(load_weight(w3, "w3", q))
            page.append(load_page(q))
        idx3 = load_list(offs3, "idx3")
        wo_raw = keep([P, N], I32, "wo_raw")
        nc.sync.dma_start(out=wo_raw[:], in_=wo_words[0].rearrange("p n i -> p (n i)").bitcast(I32))

        def fetch_before(q):
            neg = keep([P, M], F32, "minus_before%d" % q)
            for half in range(2):
                nc.vector.tensor_scalar(
                    out=neg[:, HALF * half : HALF * (half + 1)],
                    in0=page[q][:].indirect(idx4[:, 32 * half : 32 * (half + 1)]),
                    scalar1=-1.0, scalar2=0.0, op0=MULT, op1=ADD,
                )
            return neg

        minus_before = []

        v_sc = keep([P, S], U8, "v_sc")
        nc.vector.tensor_copy(v_sc[:], tab_sc[:].indirect(idx1[:]))
        nc.gpsimd.dma_start(out=v_sc1[0 : P - 4, :].bitcast(I32), in_=v_sc[4:P, :].bitcast(I32))
        v_w = []
        for a in range(PASSES):
            tile = keep([P, S], U32, "v_w%d" % a)
            pieces = 1 if a == 0 else 2
            for n in range(pieces):
                width = S // pieces
                nc.vector.tensor_copy(
                    tile[:, width * n : width * (n + 1)],
                    tab[a][:].bitcast(U32).indirect(idx1[:, width // 16 * n : width // 16 * (n + 1)]),
                )
            v_w.append(tile)

        def v_operand(a, cols, partner):
            scale = v_sc1[:, cols] if (a == 1 and partner.dtype == FP4X4) else v_sc[4 * a : P, cols]
            return v_w[a][:, cols].bitcast(FP8X4), scale

        def quantise_weight(raw, name, q, on_vector):
            rounded = keep([P, PASSES, P, 4], BF16, "%s_bf%d" % (name, q))
            dst = rounded[:].rearrange("p a (c i) j -> p a c j i", i=2)
            src = raw[:].rearrange("p a j (c i) -> p a c j i", i=2)
            if on_vector:
                nc.vector.tensor_copy(out=dst, in_=src)
            else:
                nc.scalar.copy(out=dst, in_=src)
            codes = keep([P, PASSES * P], U32, "%s_codes%d" % (name, q))
            scales = keep([P, PASSES * P], U8, "%s_scales%d" % (name, q))
            nc.vector.quantize_mx(
                out=codes[:].bitcast(FP8X4), scales=scales[:], in_=rounded[:].rearrange("p a c j -> p (a c j)")
            )
            return [(codes[:, P * a : P * (a + 1)].bitcast(FP8X4), scales[:, P * a : P * (a + 1)]) for a in range(PASSES)]

        def w2_operand(q):
            return [
                (w2_w[:, a, 2 * P * q : 2 * P * (q + 1)].bitcast(FP4X4), w2_sc[:, a, P * q : P * (q + 1)])
                for a in range(PASSES)
            ]

        def product_rows(out, weight, j0, width):
            cols = slice(j0, j0 + width)
            for a in range(PASSES):
                codes, scale = v_operand(a, cols, weight[a][0])
                nc.tensor.matmul_mx(
                    out=out[:, 0:width], lhsT=weight[a][0], lhsT_scale=weight[a][1], rhs=codes, rhs_scale=scale,
                    start=(a == 0), stop=(a == PASSES - 1),
                )

        def product_turned(out, weight, j0):
            for jt in range(HALF // P):
                cols = slice(j0 + P * jt, j0 + P * (jt + 1))
                for a in range(PASSES):
                    codes, scale = v_operand(a, cols, weight[a][0])
                    nc.tensor.matmul_mx(
                        out=out[:, P * jt : P * (jt + 1)], lhsT=codes, lhsT_scale=scale,
                        rhs=weight[a][0], rhs_scale=weight[a][1], start=(a == 0), stop=(a == PASSES - 1),
                    )

        def transposed_sum(out, parts):
            for n, (block, src) in enumerate(parts):
                nc.tensor.matmul(
                    out=out[:, P * block : P * (block + 1)], lhsT=src, rhs=ident[:], is_transpose=True,
                    start=(n == 0), stop=(n == len(parts) - 1),
                )

        def inner_tanh(q, j0, width, w1_q):
            first, second = bank("first"), bank("second")
            if width < HALF and j0 > 0:
                ga = keep([P, width], F32, "ga_late", tag="minus_before0")
            else:
                ga = turn([P, width], F32, "other" if (q == 0 and j0 > 0) else "ga")
            other = turn([P, width], F32, "other")
            b = turn([P, width], F32, "b")
            if width < HALF:
                product_rows(first, w1_q, j0, width)
                product_rows(second, w2_operand(q), j0, width)
                nc.scalar.activation(out=ga[:], in_=first[:, 0:width], func=ACT.Gelu_apprx_tanh)
                nc.vector.tensor_tensor(other[:], second[:, 0:width], ga[:], ADD)
                nc.scalar.activation(out=b[:], in_=other[:], func=ACT.Tanh)
            else:
                product_turned(first, w1_q, j0)
                product_turned(second, w2_operand(q), j0)
                nc.scalar.activation(out=ga[:], in_=first[:], func=ACT.Gelu_apprx_tanh)
                nc.scalar.copy(out=other[:], in_=second[:])
                total = bank("total")
                blocks = range(HALF // P)
                transposed_sum(
                    total,
                    [(jt, ga[:, P * jt : P * (jt + 1)]) for jt in blocks]
                    + [(jt, other[:, P * jt : P * (jt + 1)]) for jt in blocks],
                )
                nc.scalar.activation(out=b[:], in_=total[:], func=ACT.Tanh)
            return b

        after = [None] * CHUNKS
        after_early = keep([P, ROW_TILES, EARLY * CHUNK], F32, "after_early", tag="tab0")
        for c in range(EARLY):
            after[c] = after_early[:, :, CHUNK * c : CHUNK * (c + 1)]
        x_turned = [keep([P, CHUNK // P, 2, P, 2], BF16, "x_turned%d" % c) for c in range(EARLY)]

        def fetch_after(dst, m0, width, q):
            nc.vector.tensor_copy(dst, page[q][:].indirect(idx3[:, m0 // 16 : (m0 + width) // 16]))

        def difference_part(c, mt_list, q_list, tag):
            total = bank(tag)
            blocks = [(mt, q) for mt in mt_list for q in q_list]
            transposed_sum(
                total,
                [(n, minus_before[q][:, CHUNK * c + P * mt : CHUNK * c + P * (mt + 1)]) for n, (mt, q) in enumerate(blocks)]
                + [(n, after[c][:, q, P * mt : P * (mt + 1)]) for n, (mt, q) in enumerate(blocks)],
            )
            nc.scalar.copy(
                out=x_turned[c][:, mt_list[0] : mt_list[-1] + 1, :, 32 * q_list[0] : 32 * (q_list[-1] + 1), :],
                in_=total[:, 0 : P * len(blocks)].rearrange("m (mt p u e) -> m mt u p e", mt=len(mt_list), u=2, e=2),
            )

        def difference_all(c):
            x_turned.append(keep([P, CHUNK // P, 2, P, 2], BF16, "x_turned%d" % c, tag="x_turned%d" % (EARLY - 1)))
            for mt in range(CHUNK // P):
                difference_part(c, [mt], list(range(ROW_TILES)), "third" if c == EARLY else "total")

        w1_q = [quantise_weight(w1_raw[0], "w1", 0, False)]
        wo_sc = keep([P, N], U8, "wo_sc")
        nc.vector.tensor_copy(
            out=wo_sc[:].rearrange("p (g t c i) -> p g c t i", g=GROUPS, t=4, i=16),
            in_=wo_sc_raw[:].rearrange("p (g c i t) -> p g c t i", g=GROUPS, t=4, i=16),
        )
        w3_q = [quantise_weight(w3_raw[0], "w3", 0, True)]
        gain_bank = bank("total")
        nc.tensor.transpose(gain_bank[:, 0:P], gain_rows[:], ident[:])
        gain_col = keep([P, ROW_TILES], F32, "gain_col")
        nc.scalar.copy(out=gain_col[:], in_=gain_bank[:, 0:ROW_TILES])
        for q in range(ROW_TILES):
            pieces = [(0, HALF // 2), (HALF // 2, HALF // 2), (HALF, HALF)] if q == 0 else [(0, HALF), (HALF, HALF)]

            def products(j0, width):
                b = inner_tanh(q, j0, width, w1_q[q])
                third = bank("third")
                product_rows(third, w3_q[q], j0, width)
                return b, third

            def put(group, held_back):
                j0, width = group[0][0], sum(piece[1] for piece in group)
                if held_back:
                    w1_q.append(quantise_weight(w1_raw[q + 1], "w1", q + 1, False))
                    w3_q.append(quantise_weight(w3_raw[q + 1], "w3", q + 1, False))
                    h = keep([P, width], F32, "h_late%d" % q, tag="w1_bf%d" % (q + 1))
                elif width == S:
                    h = keep([P, width], F32, "h_late%d" % q, tag="tab1")
                else:
                    h = turn([P, width], F32, "h")
                for start, cols, b, third in group:
                    nc.vector.scalar_tensor_tensor(
                        out=h[:, start - j0 : start - j0 + cols], in0=b[:], scalar=gain_col[:, q : q + 1],
                        in1=third[:, 0:cols], op0=MULT, op1=ADD,
                    )
                nc.vector.tensor_tensor(
                    page[q][:].indirect(idx2[:, j0 // 16 : (j0 + width) // 16]), h[:], wgs_sb[:, j0 : j0 + width], MULT
                )

            made = [piece + products(*piece) for piece in pieces[:2]]
            if q > 0:
                fetch_after(after_early[:, q - 1, :], 0, EARLY * CHUNK, q - 1)
            minus_before.append(fetch_before(q))
            if q >= 2:
                put(made, q + 1 < ROW_TILES)
            else:
                for n in range(len(pieces)):
                    put([made[n]], n == 1 - q)
                    if n + 2 < len(pieces):
                        made.append(pieces[n + 2] + products(*pieces[n + 2]))
            if q == 1:
                wo_w = keep([P, N], I32, "wo_w")
                nc.vector.tensor_copy(
                    out=wo_w[:].rearrange("p (g t c i) -> p g c t i", g=GROUPS, t=4, i=4),
                    in_=wo_raw[:].rearrange("p (g c i t) -> p g c t i", g=GROUPS, t=4, i=4),
                )
        for c in range(EARLY):
            for mt in range(CHUNK // P):
                difference_part(c, [mt], list(range(ROW_TILES - 1)), "third")
        for c in range(EARLY):
            fetch_after(after[c][:, ROW_TILES - 1, :], CHUNK * c, CHUNK, ROW_TILES - 1)
            difference_part(c, list(range(CHUNK // P)), [ROW_TILES - 1], "total")

        y_sc = keep([P, GROUPS, M], U8, "y_sc")
        raw_tags = ["w%d_raw%d" % (w, q) for q in range(ROW_TILES) for w in (1, 3)]

        def late_chunk(c, tag):
            after[c] = keep([P, ROW_TILES, CHUNK], F32, "after%d" % c, tag=tag)
            for q in range(ROW_TILES):
                fetch_after(after[c][:, q, :], CHUNK * c, CHUNK, q)

        def quantise_x(c):
            if c >= EARLY:
                difference_all(c)
            pairs = bank(("first", "second", "third", "third")[c])
            words = x_turned[c][:].rearrange("m mt u p e -> m (mt u p e)").bitcast(F32)
            for n in range(2 * CHUNK // P):
                nc.tensor.transpose(pairs[:, P * n : P * (n + 1)], words[:, P * n : P * (n + 1)], ident[:])
            x_bf = keep([P, CHUNK * 4], BF16, "x_bf%d" % c)
            nc.scalar.copy(
                out=x_bf[:].bitcast(F32).rearrange("p (mt m u) -> p mt m u", u=2, m=P),
                in_=pairs[:].rearrange("p (mt u m) -> p mt m u", u=2, m=P),
            )
            codes = turn([P, CHUNK], U32, "x_codes")
            scales = turn([P, CHUNK], U8, "x_scales")
            nc.vector.quantize_mx(out=codes[:].bitcast(FP8X4), scales=scales[:], in_=x_bf[:])
            return codes, scales

        def last_product(c, codes, scales):
            cols = slice(CHUNK * c, CHUNK * (c + 1))
            for g in range(GROUPS):
                y = keep([P, 4, CHUNK], F32, "y%d_%d" % (c, g), tag=raw_tags[GROUPS * c + g])
                for pair in range(2):
                    acc = bank("first" if pair == 0 else "second")
                    for n in range(2):
                        n0 = 512 * g + P * (2 * pair + n)
                        nc.tensor.matmul_mx(
                            out=acc[:, CHUNK * n : CHUNK * (n + 1)],
                            lhsT=wo_w[:, n0 : n0 + P].bitcast(FP8X4), lhsT_scale=wo_sc[:, n0 : n0 + P],
                            rhs=codes[:].bitcast(FP8X4), rhs_scale=scales[:], start=True, stop=True,
                        )
                    nc.scalar.copy(out=y[:, 2 * pair : 2 * pair + 2, :].rearrange("p t m -> p (t m)"), in_=acc[:])
                nc.sync.dma_start(
                    out=out_0[512 * g : 512 * (g + 1), cols].rearrange("(p t) m -> p t m", t=4), in_=y[:]
                )
                if c % 2 == 0:
                    y_bf[g] = turn([P, 2 * CHUNK, 4], BF16, "y_bf")
                nc.vector.tensor_copy(
                    out=y_bf[g][:, CHUNK * (c % 2) : CHUNK * (c % 2 + 1), :].rearrange("p (c i) t -> p c t i", i=2),
                    in_=y[:].rearrange("p t (c i) -> p c t i", i=2),
                )
                if c % 2 == 1:
                    both = slice(CHUNK * (c - 1), CHUNK * (c + 1))
                    y_codes = keep([P, 2 * CHUNK], U32, "y_codes%d_%d" % (c, g))
                    nc.vector.quantize_mx(
                        out=y_codes[:].bitcast(FP8X4), scales=y_sc[:, g, both],
                        in_=y_bf[g][:].rearrange("p m t -> p (m t)"),
                    )
                    nc.sync.dma_start(
                        out=out_1[g, :, both, :].rearrange("p m t -> p (m t)").bitcast(I32), in_=y_codes[:].bitcast(I32)
                    )

        y_bf = [None] * GROUPS
        late_chunk(EARLY, "wgs_sb")
        quantised = []
        for c in range(CHUNKS):
            quantised.append(quantise_x(c))
            if c == 0:
                late_chunk(EARLY + 1, "x_bf0")
            if c >= 1:
                last_product(c - 1, *quantised[c - 1])
        last_product(CHUNKS - 1, *quantised[CHUNKS - 1])
        for quad in range(4):
            (nc.sync if quad % 2 else nc.scalar).dma_start(
                out=out_2[:, 4 * quad : 4 * quad + 4, :].rearrange("g r m -> r g m").bitcast(I32),
                in_=y_sc[32 * quad : 32 * quad + 4, :, :].bitcast(I32),
            )
